import numpy as np
import ml_dtypes


def mxq(x, axis, fmt="e4m3"):
    dtype, down = {"e4m3": (ml_dtypes.float8_e4m3fn, 7), "e5m2": (ml_dtypes.float8_e5m2, 14)}[fmt]
    v = np.moveaxis(np.asarray(x, np.float32).astype(ml_dtypes.bfloat16).astype(np.float64), axis, -1)
    blocks = v.reshape(v.shape[:-1] + (-1, 32))
    amax = np.abs(blocks).max(-1, keepdims=True)
    byte = np.maximum(np.where(amax > 0, np.frexp(amax)[1] - 1 + 127, 0) - down, 1)
    scale = np.exp2(byte - 127.0)
    codes = (blocks / scale).astype(np.float32).astype(dtype).astype(np.float64)
    return np.moveaxis((codes * scale).reshape(v.shape), -1, axis)


WIDE = False


def mx_kscale(k):
    if not WIDE:
        return np.ones(k)
    levels = np.array([10, -10, 5, -5, 0])
    if k % 512:
        return np.exp2(np.random.permutation(np.resize(levels, k // 32))).repeat(32)
    a = np.empty((k // 512, 16))
    for p in range(k // 512):
        a[p, :8] = np.random.permutation(np.resize(levels, 8))
        for g in range(8):
            far = levels[np.abs(levels - a[p, g]) >= 10]
            a[p, g + 8] = far[np.random.randint(len(far))]
    return np.exp2(a.ravel()).repeat(32)


def f64(x):
    return np.asarray(x).astype(np.float64)


def striped8(idx):
    return np.asarray(idx).reshape(8, -1, 16).transpose(0, 2, 1).reshape(128, -1).astype(np.uint16)


def unstriped8(offs):
    return offs.reshape(8, 16, -1).transpose(0, 2, 1).reshape(8, -1).astype(np.int64)


def pick8(x, idx, run):
    r = np.arange(len(x))
    return x[r[:, None], idx[r % (8 * run) // run]]


E2M1 = np.array([0.0, 0.5, 1.0, 1.5, 2.0, 3.0, 4.0, 6.0, -0.0, -0.5, -1.0, -1.5, -2.0, -3.0, -4.0, -6.0])


def pack_weight(w, fmt):
    k, n = w.shape
    w = f64(np.asarray(w, np.float32).astype(ml_dtypes.bfloat16)).reshape(k // 32, 32, n)
    amax = np.abs(w).max(1)
    if fmt == "e4m3":
        byte = np.frexp(amax)[1] - 1 + 127 - 7
    else:
        mant, ex = np.frexp(amax / 6.0)
        byte = np.where(mant > 0.5, ex, ex - 1) + 127
    byte = np.clip(np.where(amax > 0, byte, 1), 1, 254)
    scaled = (w * np.exp2(127.0 - byte)[:, None, :]).reshape(k, n).astype(np.float32)
    by_word = np.ascontiguousarray(scaled.reshape(k // 512, 128, 4, n).transpose(0, 1, 3, 2))
    if fmt == "e4m3":
        words = by_word.astype(ml_dtypes.float8_e4m3fn).view(np.uint8)
    else:
        c = by_word.astype(ml_dtypes.float4_e2m1fn).view(np.uint8) & 0xF
        words = (c[..., 0::2] | (c[..., 1::2] << 4)).reshape(k // 512, 128, 2 * n)
    return np.ascontiguousarray(words), np.ascontiguousarray(byte.astype(np.uint8).reshape(k // 512, 16, n))


def unpack_weight(words, scales, fmt):
    g, _, n = scales.shape
    words = np.ascontiguousarray(words).reshape(g, 128, n, -1)
    if fmt == "e4m3":
        vals = words.view(ml_dtypes.float8_e4m3fn).astype(np.float64)
    else:
        nib = np.empty((g, 128, n, 4), np.uint8)
        nib[..., 0::2] = words & 0xF
        nib[..., 1::2] = words >> 4
        vals = E2M1[nib]
    vals = vals * np.repeat(np.exp2(scales.astype(np.float64) - 127.0), 8, axis=1)[..., None]
    return vals.transpose(0, 1, 3, 2).reshape(g * 512, n)


D, T, I, Q = 512, 1024, 512, 128


def setup_inputs():
    n = np.random.standard_normal
    idx = np.stack([np.random.permutation(T)[:I] for _ in range(8)])
    idx2 = np.stack([np.random.permutation(T)[:I] for _ in range(8)])
    idx3 = np.stack([np.random.permutation(T)[:I] for _ in range(8)])
    idx4 = np.stack([np.random.permutation(T)[:I] for _ in range(8)])
    fd = mx_kscale(D)
    keysp = pack_weight(n((D, T)) / fd[:, None], "e2m1")
    return {
        "query": (n((D, Q)) * 1.0 / np.sqrt(D) * fd[:, None]).astype(np.float32),
        "keys_words": keysp[0],
        "keys_scales": keysp[1],
        "offs": striped8(idx),
        "offs2": striped8(idx2),
        "offs3": striped8(idx3),
        "offs4": striped8(idx4),
    }


def reference(query, keys_words, keys_scales, offs, offs2, offs3, offs4):
    idx = unstriped8(offs)
    idx2 = unstriped8(offs2)
    idx3 = unstriped8(offs3)
    idx4 = unstriped8(offs4)
    keysu = unpack_weight(keys_words, keys_scales, "e2m1")
    queryq = mxq(f64(query), 0, "e4m3")
    a = queryq.T @ keysu
    w = np.maximum(pick8(a, idx, 16), pick8(a, idx2, 16))
    f1 = np.zeros((Q, T))
    f1[np.arange(Q)[:, None], idx3[np.arange(Q) % 128 // 16]] = w
    cc = a + f1
    tc2 = np.max(cc, axis=1, keepdims=True)
    y = np.exp(pick8(cc, idx4, 16) - tc2)
    return y

from contextlib import ExitStack

import concourse.mybir as mybir

D, T, SLOTS, Q = 512, 1024, 512, 128
FLOPS = 2 * D * T * Q

F32 = mybir.dt.float32
BF16 = mybir.dt.bfloat16
I32 = mybir.dt.int32
U32 = mybir.dt.uint32
U16 = mybir.dt.uint16
U8 = mybir.dt.uint8
FP8X4 = mybir.dt.float8_e4m3fn_x4
FP4X4 = mybir.dt.float4_e2m1fn_x4
ALU = mybir.AluOpType
ACT = mybir.ActivationFunctionType

P = 128
PACK = 4
STRIPE = 16
WIDTHS = (256, 256, 256, 128, 128)
FIRST = 128
HALF = SLOTS // 2


def entries(offsets, first, count):
    return offsets[:, first // STRIPE : (first + count) // STRIPE]


def tile_attend_bestahead_one_kernel(tc, query, keys_words, keys_scales, offs, offs2, offs3, offs4, out):
    nc = tc.nc
    with ExitStack() as ctx:
        lists = ctx.enter_context(tc.tile_pool(name="lists", bufs=1))
        sb = ctx.enter_context(tc.tile_pool(name="sb", bufs=1))
        psum = ctx.enter_context(tc.psum_pool(name="psum", bufs=1))

        k_scales = sb.tile([P, T], U8, name="k_scales", align_bytes=64)
        nc.vector.memset(k_scales[:].bitcast(I32), 0)

        q_raw = sb.tile([P, PACK, Q], F32, name="q_raw")
        nc.sync.dma_start(q_raw[:], query.rearrange("(p j) q -> p j q", j=PACK))
        k_words = sb.tile([P, 2 * T], U8, name="k_words", align_bytes=64)
        nc.sync.dma_start(k_words[:].bitcast(I32), keys_words[0].bitcast(I32))
        for quad in range(4):
            nc.sync.dma_start(
                k_scales[32 * quad : 32 * quad + 4, :].bitcast(I32),
                keys_scales[0, 4 * quad : 4 * quad + 4, :].bitcast(I32),
            )
        idx1 = lists.tile([P, SLOTS // STRIPE], U16, name="idx1")
        nc.sync.dma_start(idx1[:], offs)
        idx2 = lists.tile([P, SLOTS // STRIPE], U16, name="idx2")
        nc.sync.dma_start(idx2[:], offs2)
        idx3 = lists.tile([P, SLOTS // STRIPE], U16, name="idx3")
        nc.sync.dma_start(idx3[:], offs3)
        idx4 = lists.tile([P, SLOTS // STRIPE], U16, name="idx4")
        nc.sync.dma_start(idx4[:], offs4)

        f1 = sb.tile([P, T], F32, name="f1")
        nc.vector.memset(f1[:], 0.0)

        q_bf = sb.tile([P, Q, PACK], BF16, name="q_bf", align_bytes=64)
        q_codes = sb.tile([P, Q], U32, name="q_codes", align_bytes=64)
        q_scales = sb.tile([P, Q], U8, name="q_scales", align_bytes=64)
        q_halves = [slice(0, Q // 2), slice(Q // 2, Q)]
        for rows in q_halves:
            nc.vector.tensor_copy(
                q_bf[:, rows, :].rearrange("p (c i) j -> p c j i", i=4),
                q_raw[:, :, rows].rearrange("p j (c i) -> p c j i", i=4),
            )
        for rows in q_halves:
            nc.vector.quantize_mx(
                out=q_codes[:, rows].bitcast(FP8X4),
                scales=q_scales[:, rows],
                in_=q_bf[:, rows, :].rearrange("p q j -> p (q j)"),
            )

        a = sb.tile([P, T], F32, name="a")
        for n, width in enumerate(WIDTHS):
            cols = slice(sum(WIDTHS[:n]), sum(WIDTHS[: n + 1]))
            bank = psum.tile([P, width], F32, name="bank%d" % n)
            nc.tensor.matmul_mx(
                out=bank[:],
                lhsT=q_codes[:].bitcast(FP8X4),
                lhsT_scale=q_scales[:],
                rhs=k_words[:, 2 * cols.start : 2 * cols.stop].bitcast(FP4X4),
                rhs_scale=k_scales[:, cols],
                start=True,
                stop=True,
            )
            if n % 2 == 0:
                nc.scalar.copy(a[:, cols], bank[:])
            else:
                nc.vector.tensor_copy(a[:, cols], bank[:])

        g1 = [sb.tile([P, HALF], F32, name="g1_%d" % h) for h in range(2)]
        g2 = [sb.tile([P, HALF], F32, name="g2_%d" % h) for h in range(2)]
        w = sb.tile([P, SLOTS], F32, name="w")
        nc.vector.tensor_copy(g1[0][:], a[:].indirect(entries(idx1, 0, HALF)))
        nc.scalar.activation(g2[0][:], a[:].indirect(entries(idx2, 0, HALF)), ACT.Copy)
        nc.scalar.activation(g1[1][:], a[:].indirect(entries(idx1, HALF, HALF)), ACT.Copy)
        nc.scalar.activation(g2[1][:], a[:].indirect(entries(idx2, HALF, HALF)), ACT.Copy)
        nc.vector.tensor_tensor(w[:, :FIRST], g1[0][:, :FIRST], g2[0][:, :FIRST], ALU.max)
        nc.vector.tensor_tensor(w[:, FIRST:HALF], g1[0][:, FIRST:], g2[0][:, FIRST:], ALU.max)
        nc.vector.tensor_copy(f1[:].indirect(entries(idx3, 0, FIRST)), w[:, :FIRST])
        nc.vector.tensor_tensor(w[:, HALF:], g1[1][:], g2[1][:], ALU.max)
        nc.vector.tensor_copy(f1[:].indirect(entries(idx3, FIRST, SLOTS - FIRST)), w[:, FIRST:])

        cc = sb.tile([P, T], F32, name="cc")
        nc.vector.tensor_tensor(cc[:], a[:], f1[:], ALU.add)
        neg_top = sb.tile([P, 1], F32, name="neg_top")
        nc.vector.tensor_reduce(neg_top[:], cc[:], mybir.AxisListType.X, ALU.max, negate=True)

        for h in range(2):
            y = sb.tile([P, HALF], F32, name="y_%d" % h)
            nc.scalar.activation(y[:], cc[:].indirect(entries(idx4, h * HALF, HALF)), ACT.Exp, bias=neg_top[:])
            nc.sync.dma_start(out[:, h * HALF : (h + 1) * HALF], y[:])
